import numpy as np
import ml_dtypes


def mxq(x, axis, fmt="e4m3"):
    dtype, down = {"e4m3": (ml_dtypes.float8_e4m3fn, 7), "e5m2": (ml_dtypes.float8_e5m2, 14)}[fmt]
    v = np.moveaxis(np.asarray(x, np.float32).astype(ml_dtypes.bfloat16).astype(np.float64), axis, -1)
    blocks = v.reshape(v.shape[:-1] + (-1, 32))
    amax = np.abs(blocks).max(-1, keepdims=True)
    byte = np.maximum(np.where(amax > 0, np.frexp(amax)[1] - 1 + 127, 0) - down, 1)
    scale = np.exp2(byte - 127.0)
    codes = (blocks / scale).astype(np.float32).astype(dtype).astype(np.float64)
    return np.moveaxis((codes * scale).reshape(v.shape), -1, axis)


WIDE = False


def mx_kscale(k):
    if not WIDE:
        return np.ones(k)
    levels = np.array([10, -10, 5, -5, 0])
    if k % 512:
        return np.exp2(np.random.permutation(np.resize(levels, k // 32))).repeat(32)
    a = np.empty((k // 512, 16))
    for p in range(k // 512):
        a[p, :8] = np.random.permutation(np.resize(levels, 8))
        for g in range(8):
            far = levels[np.abs(levels - a[p, g]) >= 10]
            a[p, g + 8] = far[np.random.randint(len(far))]
    return np.exp2(a.ravel()).repeat(32)


def f64(x):
    return np.asarray(x).astype(np.float64)


def striped(idx):
    return np.tile(idx.reshape(-1, 16).T, (8, 1)).astype(np.uint16)


def unstriped(offs):
    return offs[:16].T.reshape(-1).astype(np.int64)


E2M1 = np.array([0.0, 0.5, 1.0, 1.5, 2.0, 3.0, 4.0, 6.0, -0.0, -0.5, -1.0, -1.5, -2.0, -3.0, -4.0, -6.0])


def pack_weight(w, fmt):
    k, n = w.shape
    w = f64(np.asarray(w, np.float32).astype(ml_dtypes.bfloat16)).reshape(k // 32, 32, n)
    amax = np.abs(w).max(1)
    if fmt == "e4m3":
        byte = np.frexp(amax)[1] - 1 + 127 - 7
    else:
        mant, ex = np.frexp(amax / 6.0)
        byte = np.where(mant > 0.5, ex, ex - 1) + 127
    byte = np.clip(np.where(amax > 0, byte, 1), 1, 254)
    scaled = (w * np.exp2(127.0 - byte)[:, None, :]).reshape(k, n).astype(np.float32)
    by_word = np.ascontiguousarray(scaled.reshape(k // 512, 128, 4, n).transpose(0, 1, 3, 2))
    if fmt == "e4m3":
        words = by_word.astype(ml_dtypes.float8_e4m3fn).view(np.uint8)
    else:
        c = by_word.astype(ml_dtypes.float4_e2m1fn).view(np.uint8) & 0xF
        words = (c[..., 0::2] | (c[..., 1::2] << 4)).reshape(k // 512, 128, 2 * n)
    return np.ascontiguousarray(words), np.ascontiguousarray(byte.astype(np.uint8).reshape(k // 512, 16, n))


def unpack_weight(words, scales, fmt):
    g, _, n = scales.shape
    words = np.ascontiguousarray(words).reshape(g, 128, n, -1)
    if fmt == "e4m3":
        vals = words.view(ml_dtypes.float8_e4m3fn).astype(np.float64)
    else:
        nib = np.empty((g, 128, n, 4), np.uint8)
        nib[..., 0::2] = words & 0xF
        nib[..., 1::2] = words >> 4
        vals = E2M1[nib]
    vals = vals * np.repeat(np.exp2(scales.astype(np.float64) - 127.0), 8, axis=1)[..., None]
    return vals.transpose(0, 1, 3, 2).reshape(g * 512, n)


def gelu(v):
    return 0.5 * v * (1.0 + np.tanh(np.sqrt(2.0 / np.pi) * (v + 0.044715 * v**3)))


K, T, S, S2 = 1024, 2048, 512, 512


def setup_inputs():
    n = np.random.standard_normal
    s = mx_kscale(K)[:, None]
    d = {}
    d["tab_words"], d["tab_scales"] = pack_weight(n((K, T)) * s, "e4m3")
    d["offs"] = striped(np.random.permutation(T)[:S])
    d["offs2"] = striped(np.random.permutation(T)[:S2])
    d["w4_words"], d["w4_scales"] = pack_weight(1.4 * n((K, K)) / K / s / s.T, "e2m1")
    d["wf"] = (1.4 * n((K, K)) / K / s / s.T).astype(np.float32)
    d["ga"] = np.exp(0.3 * n(S2)).astype(np.float32)
    d["prior"] = n((S2, S)).astype(np.float32)
    return d


def reference(tab_words, tab_scales, offs, offs2, w4_words, w4_scales, wf, ga, prior):
    TW = unpack_weight(tab_words, tab_scales, "e4m3")
    v = TW[:, unstriped(offs)]
    v2 = TW[:, unstriped(offs2)]
    w4 = unpack_weight(w4_words, w4_scales, "e2m1")
    wq = mxq(f64(wf), 0, "e4m3")
    ha = np.abs(w4.T @ v + wq.T @ v)
    hb = np.maximum(w4.T @ v2 + wq.T @ v2, 0.0)
    e1 = v2.T @ mxq(ha, 0, "e4m3")
    e2 = mxq(hb, 0, "e4m3").T @ v
    low = np.minimum(e1 * f64(ga)[:, None], e2 + f64(prior))
    return 1.0 / (1.0 + np.exp(-low))

@@ -1,0 +1,261 @@
+from contextlib import ExitStack
+
+import concourse.mybir as mybir
+
+K, T, S = 1024, 2048, 512
+FLOPS = 5368709120
+
+F32 = mybir.dt.float32
+BF16 = mybir.dt.bfloat16
+I32 = mybir.dt.int32
+U32 = mybir.dt.uint32
+U16 = mybir.dt.uint16
+U8 = mybir.dt.uint8
+FP8X4 = mybir.dt.float8_e4m3fn_x4
+FP4X4 = mybir.dt.float4_e2m1fn_x4
+ACT = mybir.ActivationFunctionType
+ALU = mybir.AluOpType
+
+P = 128
+PASS = 512
+
+
+def tile_list_mutual_appeal_scores_kernel(tc, tab_words, tab_scales, offs, offs2, w4_words, w4_scales, wf, ga, prior, out):
+    nc = tc.nc
+    with ExitStack() as ctx:
+        keep = ctx.enter_context(tc.tile_pool(name="keep", bufs=1))
+        psum = ctx.enter_context(tc.psum_pool(name="psum", bufs=1))
+
+        def tile(shape, dtype, name):
+            return keep.tile(shape, dtype, name=name, align_bytes=64)
+
+        def bank(i):
+            return psum.tile([P, PASS], F32, name="bank%d" % i, tag="bank%d" % i)
+
+        lists = [keep.tile([P, S // 16], U16, name="list%d" % l) for l in range(2)]
+        tab_s = keep.tile([P, T], U8, name="tab_s", tag="shared", align_bytes=64)
+        w4s_raw = tile([P, K], U8, "w4s_raw")
+        gs1 = tile([P, 2 * S], U8, "gs1")
+        w4s1 = tile([P, K], U8, "w4s1")
+
+        nc.gpsimd.memset(tab_s[:].bitcast(I32), 0)
+        nc.vector.memset(gs1[:].bitcast(I32), 0)
+        nc.vector.memset(w4s1[:].bitcast(I32), 0)
+        nc.vector.memset(w4s_raw[:].bitcast(I32), 0)
+        nc.sync.dma_start(lists[0][:], offs)
+        nc.sync.dma_start(lists[1][:], offs2)
+        tab_rows = tab_scales.rearrange("a (q r) t -> r q a t", r=4)
+        w4_rows = w4_scales.rearrange("a (q r) t -> r q a t", r=4)
+        for r in range(4):
+            nc.scalar.dma_start(tab_s[r:P:16, :].bitcast(I32), tab_rows[r].bitcast(I32))
+        for r in range(4):
+            queue = nc.scalar if r < 2 else nc.gpsimd
+            queue.dma_start(w4s_raw[r:P:16, :].bitcast(I32), w4_rows[r].bitcast(I32))
+        with tc.tile_pool(name="early", bufs=1) as early:
+            warm = early.tile([P, 8], F32, name="warm")
+            nc.vector.memset(warm[:], 0.0)
+            nc.scalar.activation(warm[:], warm[:], ACT.Sigmoid)
+        late = ctx.enter_context(tc.tile_pool(name="late", bufs=1))
+
+        w4_raw = [(keep, late)[b].tile([P, 2, 2 * PASS], U8, name="w4_raw%d" % b, align_bytes=64) for b in range(2)]
+        tab_w = [(keep, late)[a].tile([P, T], I32, name="tab_w%d" % a, align_bytes=64) for a in range(2)]
+
+        def load_w4(b):
+            src = w4_words.rearrange("a p n -> p a n")[:, :, 2 * PASS * b : 2 * PASS * (b + 1)]
+            nc.sync.dma_start(w4_raw[b][:].bitcast(I32), src.bitcast(I32))
+
+        wf_raw = [[late.tile([P, 4, PASS], F32, name="wf_raw%d%d" % (a, b), align_bytes=64) for b in range(2)] for a in range(2)]
+
+        def load_tab(a):
+            nc.sync.dma_start(tab_w[a][:], tab_words[a].rearrange("p t i -> p (t i)").bitcast(I32))
+
+        def load_wf(a, b):
+            src = wf[PASS * a : PASS * (a + 1), PASS * b : PASS * (b + 1)]
+            nc.sync.dma_start(wf_raw[a][b][:], src.rearrange("(p j) c -> p j c", j=4))
+
+        load_w4(0)
+        load_tab(0)
+        load_wf(0, 0)
+        load_tab(1)
+        load_wf(1, 0)
+        load_w4(1)
+        load_wf(0, 1)
+        load_wf(1, 1)
+        gain = late.tile([P, 4], F32, name="gain")
+        with nc.allow_non_contiguous_dma(reason="one gain for each output row"):
+            nc.sync.dma_start(gain[:], ga.rearrange("(c p) -> p c", p=P))
+        prior_sb = late.tile([P, 4, S], F32, name="prior_sb")
+        nc.sync.dma_start(prior_sb[:], prior.rearrange("(c p) j -> p c j", p=P))
+
+        w4_w = [tile([P, 2, 2 * PASS], U8, "w4_w%d" % b) for b in range(2)]
+        w4s0 = tile([P, K], U8, "w4s0")
+        gs0 = tile([P, 2 * S], U8, "gs0")
+        gw = [[None, None], [None, None]]
+        gs = [gs0, gs1]
+        w4s = [w4s0, w4s1]
+
+        def deal_w4(b):
+            nc.vector.tensor_copy(
+                w4_w[b][:].bitcast(U16).rearrange("p a (t m) -> p a m t", t=4),
+                w4_raw[b][:].bitcast(U16).rearrange("p a (m t) -> p a m t", t=4),
+            )
+
+        def gather_words(l, a):
+            tag = "shared" if l == 0 and a == 0 else "gw%d%d" % (l, a)
+            gw[l][a] = keep.tile([P, S], U32, name="gw%d%d" % (l, a), tag=tag, align_bytes=64)
+            nc.vector.tensor_copy(gw[l][a][:], tab_w[a][:].bitcast(U32).indirect(lists[l][:]))
+
+        def gather_scales(l):
+            nc.vector.tensor_copy(gs0[:, S * l : S * (l + 1)], tab_s[:].indirect(lists[l][:]))
+
+        wf_il = [[tile([P, 4 * PASS], BF16, "wf_il%d%d" % (a, b)) for b in range(2)] for a in range(2)]
+        wq_w = [[tile([P, PASS], U32, "wq_w%d%d" % (a, b)) for b in range(2)] for a in range(2)]
+        wq_s = [[tile([P, PASS], U8, "wq_s%d%d" % (a, b)) for b in range(2)] for a in range(2)]
+
+        def cast_wf(a, b, copy):
+            copy(
+                wf_il[a][b][:].rearrange("p (t m j) -> p m j t", t=4, j=4),
+                wf_raw[a][b][:].rearrange("p j (m t) -> p m j t", t=4),
+            )
+
+        def quantize_wf(a, b):
+            nc.vector.quantize_mx(out=wq_w[a][b][:].bitcast(FP8X4), scales=wq_s[a][b][:], in_=wf_il[a][b][:])
+
+        def pass_w4(acc, l, a, b, t, cols, start):
+            nc.tensor.matmul_mx(
+                out=acc,
+                lhsT=w4_w[b][:, a, 2 * P * t : 2 * P * (t + 1)].bitcast(FP4X4),
+                lhsT_scale=w4s[a][:, PASS * b + P * t : PASS * b + P * (t + 1)],
+                rhs=gw[l][a][:, cols].bitcast(FP8X4),
+                rhs_scale=gs[a][:, S * l + cols.start : S * l + cols.stop],
+                start=start,
+                stop=False,
+            )
+
+        def pass_wf(acc, l, a, b, t, cols, stop):
+            nc.tensor.matmul_mx(
+                out=acc,
+                lhsT=wq_w[a][b][:, P * t : P * (t + 1)].bitcast(FP8X4),
+                lhsT_scale=wq_s[a][b][:, P * t : P * (t + 1)],
+                rhs=gw[l][a][:, cols].bitcast(FP8X4),
+                rhs_scale=gs[a][:, S * l + cols.start : S * l + cols.stop],
+                start=False,
+                stop=stop,
+            )
+
+        funcs = [ACT.Abs, ACT.Relu]
+        h_il = [[tile([P, 4 * S], BF16, "h_il%d%d" % (l, b)) for b in range(2)] for l in range(2)]
+        hq_w = [[tile([P, S], U32, "hq_w%d%d" % (l, b)) for b in range(2)] for l in range(2)]
+        hq_s = [[tile([P, S], U8, "hq_s%d%d" % (l, b)) for b in range(2)] for l in range(2)]
+        whole = slice(0, S)
+
+        def interleave_quantize(l, b, planes):
+            nc.vector.tensor_copy(
+                h_il[l][b][:].rearrange("p (c i t) -> p c t i", i=4, t=4),
+                planes[:].rearrange("p t (c i) -> p c t i", i=4),
+            )
+            nc.vector.quantize_mx(out=hq_w[l][b][:].bitcast(FP8X4), scales=hq_s[l][b][:], in_=h_il[l][b][:])
+
+        deal_w4(0)
+        gather_scales(0)
+        gather_scales(1)
+        nc.vector.tensor_copy(
+            w4s0[:].rearrange("p (b t m) -> p b m t", b=2, t=4),
+            w4s_raw[:].rearrange("p (b m t) -> p b m t", b=2, t=4),
+        )
+        gather_words(0, 0)
+        acc = [[bank(4 * l + t) for t in range(4)] for l in range(2)]
+        for t in range(4):
+            pass_w4(acc[0][t][:], 0, 0, 0, t, whole, True)
+        gather_words(1, 0)
+        for t in range(4):
+            pass_w4(acc[1][t][:], 1, 0, 0, t, whole, True)
+        nc.scalar.dma_start(w4s1[0 : P - 16, :].bitcast(I32), w4s0[16:P, :].bitcast(I32))
+        nc.scalar.dma_start(gs1[0 : P - 16, :].bitcast(I32), gs0[16:P, :].bitcast(I32))
+        cast_wf(0, 0, nc.scalar.copy)
+        quantize_wf(0, 0)
+        for l in range(2):
+            for t in range(4):
+                pass_wf(acc[l][t][:], l, 0, 0, t, whole, False)
+        for l in range(2):
+            gather_words(l, 1)
+            for t in range(4):
+                pass_w4(acc[l][t][:], l, 1, 0, t, whole, False)
+        cast_wf(1, 0, nc.scalar.copy)
+        quantize_wf(1, 0)
+        planes = [tile([P, 4, S], BF16, "planes%d" % i) for i in range(3)]
+        for l in range(2):
+            for t in range(4):
+                pass_wf(acc[l][t][:], l, 1, 0, t, whole, True)
+                nc.scalar.activation(planes[l][:, t, :], acc[l][t][:], funcs[l])
+
+        deal_w4(1)
+        for a in range(2):
+            cast_wf(a, 1, nc.vector.tensor_copy)
+            quantize_wf(a, 1)
+        acc_a = [bank(t) for t in range(4)]
+        for t in range(4):
+            for a in range(2):
+                pass_w4(acc_a[t][:], 0, a, 1, t, whole, a == 0)
+        for t in range(4):
+            pass_wf(acc_a[t][:], 0, 0, 1, t, whole, False)
+        for t in range(4):
+            pass_wf(acc_a[t][:], 0, 1, 1, t, whole, True)
+            nc.scalar.activation(planes[2][:, t, :], acc_a[t][:], funcs[0])
+        interleave_quantize(0, 0, planes[0])
+        interleave_quantize(1, 0, planes[1])
+        interleave_quantize(0, 1, planes[2])
+
+        def traits_b(c):
+            cols = slice(P * c, P * (c + 1))
+            acc_b = bank(4 + c)
+            for t in range(4):
+                part = acc_b[:, P * t : P * (t + 1)]
+                for a in range(2):
+                    pass_w4(part, 1, a, 1, t, cols, t == 0 and a == 0)
+                for a in range(2):
+                    pass_wf(part, 1, a, 1, t, cols, t == 3 and a == 1)
+            il = h_il[1][1][:, 4 * P * c : 4 * P * (c + 1)]
+            nc.scalar.activation(il.rearrange("p (n t) -> p n t", t=4), acc_b[:].rearrange("p (t n) -> p n t", t=4), funcs[1])
+            nc.vector.quantize_mx(out=hq_w[1][1][:, cols].bitcast(FP8X4), scales=hq_s[1][1][:, cols], in_=il)
+
+        def scores(c):
+            cols = slice(P * c, P * (c + 1))
+            e1 = bank(c)
+            e2 = bank(4 + c)
+            for a in range(2):
+                nc.tensor.matmul_mx(
+                    out=e1[:],
+                    lhsT=gw[1][a][:, cols].bitcast(FP8X4),
+                    lhsT_scale=gs[a][:, S + P * c : S + P * (c + 1)],
+                    rhs=hq_w[0][a][:].bitcast(FP8X4),
+                    rhs_scale=hq_s[0][a][:],
+                    start=a == 0,
+                    stop=a == 1,
+                )
+            for a in range(2):
+                nc.tensor.matmul_mx(
+                    out=e2[:],
+                    lhsT=hq_w[1][a][:, cols].bitcast(FP8X4),
+                    lhsT_scale=hq_s[1][a][:, cols],
+                    rhs=gw[0][a][:].bitcast(FP8X4),
+                    rhs_scale=gs[a][:, 0:S],
+                    start=a == 0,
+                    stop=a == 1,
+                )
+            second = tile([P, S], F32, "second%d" % c)
+            low = tile([P, S], F32, "low%d" % c)
+            res = tile([P, S], F32, "res%d" % c)
+            nc.vector.tensor_tensor(second[:], e2[:], prior_sb[:, c, :], ALU.add)
+            nc.vector.scalar_tensor_tensor(low[:], e1[:], gain[:, c : c + 1], second[:], ALU.mult, ALU.min)
+            nc.scalar.activation(res[:], low[:], ACT.Sigmoid)
+            nc.sync.dma_start(out[cols, :], res[:])
+
+        traits_b(0)
+        traits_b(1)
+        scores(0)
+        traits_b(2)
+        scores(1)
+        traits_b(3)
+        scores(2)
+        scores(3)

@@ -33,66 +33,38 @@ def tile_list_mutual_appeal_scores_kernel(tc, tab_words, tab_scales, offs, offs2
             return psum.tile([P, PASS], F32, name="bank%d" % i, tag="bank%d" % i)
 
         lists = [keep.tile([P, S // 16], U16, name="list%d" % l) for l in range(2)]
-        tab_s = keep.tile([P, T], U8, name="tab_s", tag="shared", align_bytes=64)
-        w4s_raw = tile([P, K], U8, "w4s_raw")
         gs1 = tile([P, 2 * S], U8, "gs1")
-        w4s1 = tile([P, K], U8, "w4s1")
+        w4s_raw = keep.tile([P, 2, K], U8, name="w4s_raw", tag="shared", align_bytes=64)
 
-        nc.gpsimd.memset(tab_s[:].bitcast(I32), 0)
-        nc.vector.memset(gs1[:].bitcast(I32), 0)
-        nc.vector.memset(w4s1[:].bitcast(I32), 0)
-        nc.vector.memset(w4s_raw[:].bitcast(I32), 0)
-        nc.sync.dma_start(lists[0][:], offs)
-        nc.sync.dma_start(lists[1][:], offs2)
-        tab_rows = tab_scales.rearrange("a (q r) t -> r q a t", r=4)
-        w4_rows = w4_scales.rearrange("a (q r) t -> r q a t", r=4)
-        for r in range(4):
-            nc.scalar.dma_start(tab_s[r:P:16, :].bitcast(I32), tab_rows[r].bitcast(I32))
-        for r in range(4):
-            queue = nc.scalar if r < 2 else nc.gpsimd
-            queue.dma_start(w4s_raw[r:P:16, :].bitcast(I32), w4_rows[r].bitcast(I32))
-        with tc.tile_pool(name="early", bufs=1) as early:
-            warm = early.tile([P, 8], F32, name="warm")
-            nc.vector.memset(warm[:], 0.0)
-            nc.scalar.activation(warm[:], warm[:], ACT.Sigmoid)
-        late = ctx.enter_context(tc.tile_pool(name="late", bufs=1))
+        w4_raw = [None, None]
+        tab_w = [tile([P, T], I32, "tab_w%d" % a) for a in range(2)]
 
-        w4_raw = [(keep, late)[b].tile([P, 2, 2 * PASS], U8, name="w4_raw%d" % b, align_bytes=64) for b in range(2)]
-        tab_w = [(keep, late)[a].tile([P, T], I32, name="tab_w%d" % a, align_bytes=64) for a in range(2)]
-
-        def load_w4(b):
+        def load_w4(b, pool):
+            w4_raw[b] = pool.tile([P, 2, 2 * PASS], U8, name="w4_raw%d" % b, align_bytes=64)
             src = w4_words.rearrange("a p n -> p a n")[:, :, 2 * PASS * b : 2 * PASS * (b + 1)]
             nc.sync.dma_start(w4_raw[b][:].bitcast(I32), src.bitcast(I32))
 
-        wf_raw = [[late.tile([P, 4, PASS], F32, name="wf_raw%d%d" % (a, b), align_bytes=64) for b in range(2)] for a in range(2)]
+        wf_raw = [[None, None], [None, None]]
 
         def load_tab(a):
             nc.sync.dma_start(tab_w[a][:], tab_words[a].rearrange("p t i -> p (t i)").bitcast(I32))
 
-        def load_wf(a, b):
+        def load_wf(a, b, pool):
+            wf_raw[a][b] = pool.tile([P, 4, PASS], F32, name="wf_raw%d%d" % (a, b), align_bytes=64)
             src = wf[PASS * a : PASS * (a + 1), PASS * b : PASS * (b + 1)]
             nc.sync.dma_start(wf_raw[a][b][:], src.rearrange("(p j) c -> p j c", j=4))
 
-        load_w4(0)
-        load_tab(0)
-        load_wf(0, 0)
-        load_tab(1)
-        load_wf(1, 0)
-        load_w4(1)
-        load_wf(0, 1)
-        load_wf(1, 1)
-        gain = late.tile([P, 4], F32, name="gain")
-        with nc.allow_non_contiguous_dma(reason="one gain for each output row"):
-            nc.sync.dma_start(gain[:], ga.rearrange("(c p) -> p c", p=P))
-        prior_sb = late.tile([P, 4, S], F32, name="prior_sb")
-        nc.sync.dma_start(prior_sb[:], prior.rearrange("(c p) j -> p c j", p=P))
-
         w4_w = [tile([P, 2, 2 * PASS], U8, "w4_w%d" % b) for b in range(2)]
-        w4s0 = tile([P, K], U8, "w4s0")
         gs0 = tile([P, 2 * S], U8, "gs0")
         gw = [[None, None], [None, None]]
         gs = [gs0, gs1]
-        w4s = [w4s0, w4s1]
+        w4s = [[tile([P, PASS], U8, "w4s%d%d" % (a, b)) for b in range(2)] for a in range(2)]
+
+        def deal_w4_scales(a, b):
+            nc.vector.tensor_copy(
+                w4s[a][b][:].rearrange("p (t m) -> p m t", t=4),
+                w4s_raw[:, a, PASS * b : PASS * (b + 1)].rearrange("p (m t) -> p m t", t=4),
+            )
 
         def deal_w4(b):
             nc.vector.tensor_copy(
@@ -101,7 +73,7 @@ def tile_list_mutual_appeal_scores_kernel(tc, tab_words, tab_scales, offs, offs2
             )
 
         def gather_words(l, a):
-            tag = "shared" if l == 0 and a == 0 else "gw%d%d" % (l, a)
+            tag = "shared" if (l, a) == (1, 0) else "gw%d%d" % (l, a)
             gw[l][a] = keep.tile([P, S], U32, name="gw%d%d" % (l, a), tag=tag, align_bytes=64)
             nc.vector.tensor_copy(gw[l][a][:], tab_w[a][:].bitcast(U32).indirect(lists[l][:]))
 
@@ -125,7 +97,7 @@ def tile_list_mutual_appeal_scores_kernel(tc, tab_words, tab_scales, offs, offs2
             nc.tensor.matmul_mx(
                 out=acc,
                 lhsT=w4_w[b][:, a, 2 * P * t : 2 * P * (t + 1)].bitcast(FP4X4),
-                lhsT_scale=w4s[a][:, PASS * b + P * t : PASS * b + P * (t + 1)],
+                lhsT_scale=w4s[a][b][:, P * t : P * (t + 1)],
                 rhs=gw[l][a][:, cols].bitcast(FP8X4),
                 rhs_scale=gs[a][:, S * l + cols.start : S * l + cols.stop],
                 start=start,
@@ -156,22 +128,53 @@ def tile_list_mutual_appeal_scores_kernel(tc, tab_words, tab_scales, offs, offs2
             )
             nc.vector.quantize_mx(out=hq_w[l][b][:].bitcast(FP8X4), scales=hq_s[l][b][:], in_=h_il[l][b][:])
 
-        deal_w4(0)
-        gather_scales(0)
-        gather_scales(1)
-        nc.vector.tensor_copy(
-            w4s0[:].rearrange("p (b t m) -> p b m t", b=2, t=4),
-            w4s_raw[:].rearrange("p (b m t) -> p b m t", b=2, t=4),
-        )
+        with tc.tile_pool(name="early", bufs=1) as early:
+            tab_s = early.tile([P, T], U8, name="tab_s", align_bytes=64)
+            nc.vector.memset(tab_s[:, 0:1536].bitcast(I32), 0)
+            nc.gpsimd.memset(tab_s[:, 1536:T].bitcast(I32), 0)
+            nc.vector.memset(w4s_raw[:].bitcast(I32), 0)
+            nc.gpsimd.memset(gs1[:].bitcast(I32), 0)
+            nc.sync.dma_start(lists[0][:], offs)
+            nc.sync.dma_start(lists[1][:], offs2)
+            tab_rows = tab_scales.rearrange("a (q r) t -> r q a t", r=4)
+            w4_rows = w4_scales.rearrange("a (q r) t -> r q a t", r=4)
+            warm = tile([P, 8], F32, "warm")
+            nc.vector.memset(warm[:], 0.0)
+            nc.scalar.activation(warm[:], warm[:], ACT.Sigmoid)
+
+            load_w4(0, keep)
+            for r in range(4):
+                nc.sync.dma_start(tab_s[r:P:16, :].bitcast(I32), tab_rows[r].bitcast(I32))
+            load_tab(0)
+            for r in range(4):
+                nc.sync.dma_start(w4s_raw[r:P:32, :, :].bitcast(I32), w4_rows[r].bitcast(I32))
+            load_wf(0, 0, keep)
+            load_tab(1)
+
+            deal_w4(0)
+            gather_scales(0)
+            gather_scales(1)
+        late = ctx.enter_context(tc.tile_pool(name="late", bufs=1))
+        nc.sync.dma_start(gs1[0 : P - 16, :].bitcast(I32), gs0[16:P, :].bitcast(I32))
+        load_wf(1, 0, late)
+        load_w4(1, late)
+        load_wf(0, 1, late)
+        load_wf(1, 1, late)
+        gain = late.tile([P, 4], F32, name="gain")
+        with nc.allow_non_contiguous_dma(reason="one gain for each output row"):
+            nc.sync.dma_start(gain[:], ga.rearrange("(c p) -> p c", p=P))
+        prior_sb = late.tile([P, 4, S], F32, name="prior_sb")
+        nc.sync.dma_start(prior_sb[:], prior.rearrange("(c p) j -> p c j", p=P))
         gather_words(0, 0)
+        for b in range(2):
+            for a in range(2):
+                deal_w4_scales(a, b)
         acc = [[bank(4 * l + t) for t in range(4)] for l in range(2)]
         for t in range(4):
             pass_w4(acc[0][t][:], 0, 0, 0, t, whole, True)
         gather_words(1, 0)
         for t in range(4):
             pass_w4(acc[1][t][:], 1, 0, 0, t, whole, True)
-        nc.scalar.dma_start(w4s1[0 : P - 16, :].bitcast(I32), w4s0[16:P, :].bitcast(I32))
-        nc.scalar.dma_start(gs1[0 : P - 16, :].bitcast(I32), gs0[16:P, :].bitcast(I32))
         cast_wf(0, 0, nc.scalar.copy)
         quantize_wf(0, 0)
         for l in range(2):
@@ -222,7 +225,7 @@ def tile_list_mutual_appeal_scores_kernel(tc, tab_words, tab_scales, offs, offs2
         def scores(c):
             cols = slice(P * c, P * (c + 1))
             e1 = bank(c)
-            e2 = bank(4 + c)
+            e2 = bank(4 + c % 3)
             for a in range(2):
                 nc.tensor.matmul_mx(
                     out=e1[:],
@@ -246,10 +249,21 @@ def tile_list_mutual_appeal_scores_kernel(tc, tab_words, tab_scales, offs, offs2
             second = tile([P, S], F32, "second%d" % c)
             low = tile([P, S], F32, "low%d" % c)
             res = tile([P, S], F32, "res%d" % c)
-            nc.vector.tensor_tensor(second[:], e2[:], prior_sb[:, c, :], ALU.add)
-            nc.vector.scalar_tensor_tensor(low[:], e1[:], gain[:, c : c + 1], second[:], ALU.mult, ALU.min)
-            nc.scalar.activation(res[:], low[:], ACT.Sigmoid)
-            nc.sync.dma_start(out[cols, :], res[:])
+            if c < 3:
+                nc.vector.tensor_tensor(second[:], e2[:], prior_sb[:, c, :], ALU.add)
+                nc.vector.scalar_tensor_tensor(low[:], e1[:], gain[:, c : c + 1], second[:], ALU.mult, ALU.min)
+                nc.scalar.activation(res[:], low[:], ACT.Sigmoid)
+                nc.sync.dma_start(out[cols, :], res[:])
+            else:
+                first = tile([P, S], F32, "first")
+                nc.scalar.activation(first[:], e1[:], ACT.Sigmoid, scale=gain[:, c : c + 1])
+                parts = [slice(0, S // 2), slice(S // 2, S)]
+                for part in parts:
+                    nc.vector.tensor_tensor(second[:, part], e2[:, part], prior_sb[:, c, part], ALU.add)
+                    nc.scalar.activation(low[:, part], second[:, part], ACT.Sigmoid)
+                for part in parts:
+                    nc.vector.tensor_tensor(res[:, part], low[:, part], first[:, part], ALU.min)
+                    nc.sync.dma_start(out[cols, part], res[:, part])
 
         traits_b(0)
         traits_b(1)

@@ -50,7 +50,7 @@ def tile_list_mutual_appeal_scores_kernel(tc, tab_words, tab_scales, offs, offs2
             nc.sync.dma_start(tab_w[a][:], tab_words[a].rearrange("p t i -> p (t i)").bitcast(I32))
 
         def load_wf(a, b, pool):
-            wf_raw[a][b] = pool.tile([P, 4, PASS], F32, name="wf_raw%d%d" % (a, b), align_bytes=64)
+            wf_raw[a][b] = pool.tile([P, 4, PASS], F32, name="wf_raw%d%d" % (a, b), tag="wf_raw%d%d" % (a, b), align_bytes=64)
             src = wf[PASS * a : PASS * (a + 1), PASS * b : PASS * (b + 1)]
             nc.sync.dma_start(wf_raw[a][b][:], src.rearrange("(p j) c -> p j c", j=4))
 
@@ -62,14 +62,14 @@ def tile_list_mutual_appeal_scores_kernel(tc, tab_words, tab_scales, offs, offs2
 
         def deal_w4_scales(a, b):
             nc.vector.tensor_copy(
-                w4s[a][b][:].rearrange("p (t m) -> p m t", t=4),
-                w4s_raw[:, a, PASS * b : PASS * (b + 1)].rearrange("p (m t) -> p m t", t=4),
+                w4s[a][b][:].rearrange("p (t m) -> p t m", t=4),
+                w4s_raw[:, a, PASS * b : PASS * (b + 1)].rearrange("p (m t) -> p t m", t=4),
             )
 
         def deal_w4(b):
             nc.vector.tensor_copy(
-                w4_w[b][:].bitcast(U16).rearrange("p a (t m) -> p a m t", t=4),
-                w4_raw[b][:].bitcast(U16).rearrange("p a (m t) -> p a m t", t=4),
+                w4_w[b][:].bitcast(U16).rearrange("p a (t m) -> p a t m", t=4),
+                w4_raw[b][:].bitcast(U16).rearrange("p a (m t) -> p a t m", t=4),
             )
 
         def gather_words(l, a):
@@ -80,15 +80,17 @@ def tile_list_mutual_appeal_scores_kernel(tc, tab_words, tab_scales, offs, offs2
         def gather_scales(l):
             nc.vector.tensor_copy(gs0[:, S * l : S * (l + 1)], tab_s[:].indirect(lists[l][:]))
 
-        wf_il = [[tile([P, 4 * PASS], BF16, "wf_il%d%d" % (a, b)) for b in range(2)] for a in range(2)]
+        wf_il = [[keep.tile([P, 4 * PASS], BF16, name="wf_il%d%d" % (a, b), tag="wf_il%d%d" % (a, b), align_bytes=64) for b in range(2)] for a in range(2)]
         wq_w = [[tile([P, PASS], U32, "wq_w%d%d" % (a, b)) for b in range(2)] for a in range(2)]
         wq_s = [[tile([P, PASS], U8, "wq_s%d%d" % (a, b)) for b in range(2)] for a in range(2)]
 
-        def cast_wf(a, b, copy):
-            copy(
-                wf_il[a][b][:].rearrange("p (t m j) -> p m j t", t=4, j=4),
-                wf_raw[a][b][:].rearrange("p j (m t) -> p m j t", t=4),
-            )
+        def cast_wf(a, b, on_scalar):
+            dealt = wf_il[a][b][:].rearrange("p (t m j) -> p m j t", t=4, j=4)
+            loaded = wf_raw[a][b][:].rearrange("p j (m t) -> p m j t", t=4)
+            if on_scalar > 0:
+                nc.scalar.copy(dealt[:, 0:on_scalar, :, :], loaded[:, 0:on_scalar, :, :])
+            if on_scalar < P:
+                nc.vector.tensor_copy(dealt[:, on_scalar:P, :, :], loaded[:, on_scalar:P, :, :])
 
         def quantize_wf(a, b):
             nc.vector.quantize_mx(out=wq_w[a][b][:].bitcast(FP8X4), scales=wq_s[a][b][:], in_=wf_il[a][b][:])
@@ -116,12 +118,13 @@ def tile_list_mutual_appeal_scores_kernel(tc, tab_words, tab_scales, offs, offs2
             )
 
         funcs = [ACT.Abs, ACT.Relu]
-        h_il = [[tile([P, 4 * S], BF16, "h_il%d%d" % (l, b)) for b in range(2)] for l in range(2)]
+        h_il = [[None, None], [None, tile([P, 4 * S], BF16, "h_il11")]]
         hq_w = [[tile([P, S], U32, "hq_w%d%d" % (l, b)) for b in range(2)] for l in range(2)]
         hq_s = [[tile([P, S], U8, "hq_s%d%d" % (l, b)) for b in range(2)] for l in range(2)]
         whole = slice(0, S)
 
-        def interleave_quantize(l, b, planes):
+        def interleave_quantize(l, b, planes, pool, tag):
+            h_il[l][b] = pool.tile([P, 4 * S], BF16, name="h_il%d%d" % (l, b), tag=tag, align_bytes=64)
             nc.vector.tensor_copy(
                 h_il[l][b][:].rearrange("p (c i t) -> p c t i", i=4, t=4),
                 planes[:].rearrange("p t (c i) -> p c t i", i=4),
@@ -175,7 +178,7 @@ def tile_list_mutual_appeal_scores_kernel(tc, tab_words, tab_scales, offs, offs2
         gather_words(1, 0)
         for t in range(4):
             pass_w4(acc[1][t][:], 1, 0, 0, t, whole, True)
-        cast_wf(0, 0, nc.scalar.copy)
+        cast_wf(0, 0, 128)
         quantize_wf(0, 0)
         for l in range(2):
             for t in range(4):
@@ -184,7 +187,7 @@ def tile_list_mutual_appeal_scores_kernel(tc, tab_words, tab_scales, offs, offs2
             gather_words(l, 1)
             for t in range(4):
                 pass_w4(acc[l][t][:], l, 1, 0, t, whole, False)
-        cast_wf(1, 0, nc.scalar.copy)
+        cast_wf(1, 0, 64)
         quantize_wf(1, 0)
         planes = [tile([P, 4, S], BF16, "planes%d" % i) for i in range(3)]
         for l in range(2):
@@ -194,7 +197,7 @@ def tile_list_mutual_appeal_scores_kernel(tc, tab_words, tab_scales, offs, offs2
 
         deal_w4(1)
         for a in range(2):
-            cast_wf(a, 1, nc.vector.tensor_copy)
+            cast_wf(a, 1, 0)
             quantize_wf(a, 1)
         acc_a = [bank(t) for t in range(4)]
         for t in range(4):
@@ -205,9 +208,8 @@ def tile_list_mutual_appeal_scores_kernel(tc, tab_words, tab_scales, offs, offs2
         for t in range(4):
             pass_wf(acc_a[t][:], 0, 1, 1, t, whole, True)
             nc.scalar.activation(planes[2][:, t, :], acc_a[t][:], funcs[0])
-        interleave_quantize(0, 0, planes[0])
-        interleave_quantize(1, 0, planes[1])
-        interleave_quantize(0, 1, planes[2])
+        interleave_quantize(1, 0, planes[1], keep, "wf_il11")
+        interleave_quantize(0, 0, planes[0], late, "wf_raw11")
 
         def traits_b(c):
             cols = slice(P * c, P * (c + 1))
@@ -222,20 +224,11 @@ def tile_list_mutual_appeal_scores_kernel(tc, tab_words, tab_scales, offs, offs2
             nc.scalar.activation(il.rearrange("p (n t) -> p n t", t=4), acc_b[:].rearrange("p (t n) -> p n t", t=4), funcs[1])
             nc.vector.quantize_mx(out=hq_w[1][1][:, cols].bitcast(FP8X4), scales=hq_s[1][1][:, cols], in_=il)
 
-        def scores(c):
+        second = [tile([P, S], F32, "second%d" % c) for c in range(4)]
+
+        def second_appeal(c):
             cols = slice(P * c, P * (c + 1))
-            e1 = bank(c)
             e2 = bank(4 + c % 3)
-            for a in range(2):
-                nc.tensor.matmul_mx(
-                    out=e1[:],
-                    lhsT=gw[1][a][:, cols].bitcast(FP8X4),
-                    lhsT_scale=gs[a][:, S + P * c : S + P * (c + 1)],
-                    rhs=hq_w[0][a][:].bitcast(FP8X4),
-                    rhs_scale=hq_s[0][a][:],
-                    start=a == 0,
-                    stop=a == 1,
-                )
             for a in range(2):
                 nc.tensor.matmul_mx(
                     out=e2[:],
@@ -246,30 +239,40 @@ def tile_list_mutual_appeal_scores_kernel(tc, tab_words, tab_scales, offs, offs2
                     start=a == 0,
                     stop=a == 1,
                 )
-            second = tile([P, S], F32, "second%d" % c)
+            nc.vector.tensor_tensor(second[c][:], e2[:], prior_sb[:, c, :], ALU.add)
+
+        def scores(c):
+            cols = slice(P * c, P * (c + 1))
+            e1 = bank(c)
+            for a in range(2):
+                nc.tensor.matmul_mx(
+                    out=e1[:],
+                    lhsT=gw[1][a][:, cols].bitcast(FP8X4),
+                    lhsT_scale=gs[a][:, S + P * c : S + P * (c + 1)],
+                    rhs=hq_w[0][a][:].bitcast(FP8X4),
+                    rhs_scale=hq_s[0][a][:],
+                    start=a == 0,
+                    stop=a == 1,
+                )
             low = tile([P, S], F32, "low%d" % c)
             res = tile([P, S], F32, "res%d" % c)
-            if c < 3:
-                nc.vector.tensor_tensor(second[:], e2[:], prior_sb[:, c, :], ALU.add)
-                nc.vector.scalar_tensor_tensor(low[:], e1[:], gain[:, c : c + 1], second[:], ALU.mult, ALU.min)
-                nc.scalar.activation(res[:], low[:], ACT.Sigmoid)
-                nc.sync.dma_start(out[cols, :], res[:])
-            else:
-                first = tile([P, S], F32, "first")
-                nc.scalar.activation(first[:], e1[:], ACT.Sigmoid, scale=gain[:, c : c + 1])
-                parts = [slice(0, S // 2), slice(S // 2, S)]
-                for part in parts:
-                    nc.vector.tensor_tensor(second[:, part], e2[:, part], prior_sb[:, c, part], ALU.add)
-                    nc.scalar.activation(low[:, part], second[:, part], ACT.Sigmoid)
-                for part in parts:
-                    nc.vector.tensor_tensor(res[:, part], low[:, part], first[:, part], ALU.min)
-                    nc.sync.dma_start(out[cols, part], res[:, part])
+            width = S // 2 if c == 3 else S
+            for j in range(0, S, width):
+                part = slice(j, j + width)
+                nc.vector.scalar_tensor_tensor(low[:, part], e1[:, part], gain[:, c : c + 1], second[c][:, part], ALU.mult, ALU.min)
+                nc.scalar.activation(res[:, part], low[:, part], ACT.Sigmoid)
+                nc.sync.dma_start(out[cols, part], res[:, part])
 
         traits_b(0)
         traits_b(1)
-        scores(0)
+        interleave_quantize(0, 1, planes[2], keep, "h_il01")
         traits_b(2)
-        scores(1)
+        second_appeal(0)
         traits_b(3)
+        second_appeal(1)
+        scores(0)
+        second_appeal(2)
+        scores(1)
+        second_appeal(3)
         scores(2)
         scores(3)

@@ -17,7 +17,11 @@ ACT = mybir.ActivationFunctionType
 ALU = mybir.AluOpType
 
 P = 128
-PASS = 512
+PACK = 4
+PASS = P * PACK
+MOVING, SEATED = 0, 1
+CLEAR_ON_VECTOR = 1536
+HALF = P // 2
 
 
 def tile_list_mutual_appeal_scores_kernel(tc, tab_words, tab_scales, offs, offs2, w4_words, w4_scales, wf, ga, prior, out):
@@ -26,253 +30,225 @@ def tile_list_mutual_appeal_scores_kernel(tc, tab_words, tab_scales, offs, offs2
         keep = ctx.enter_context(tc.tile_pool(name="keep", bufs=1))
         psum = ctx.enter_context(tc.psum_pool(name="psum", bufs=1))
 
-        def tile(shape, dtype, name):
-            return keep.tile(shape, dtype, name=name, align_bytes=64)
+        def tile(shape, dtype, name, pool=keep, tag=None):
+            return pool.tile(shape, dtype, name=name, tag=tag or name, align_bytes=64)
 
         def bank(i):
             return psum.tile([P, PASS], F32, name="bank%d" % i, tag="bank%d" % i)
 
-        lists = [keep.tile([P, S // 16], U16, name="list%d" % l) for l in range(2)]
-        gs1 = tile([P, 2 * S], U8, "gs1")
-        w4s_raw = keep.tile([P, 2, K], U8, name="w4s_raw", tag="shared", align_bytes=64)
+        def block(i, width=P):
+            return slice(width * i, width * (i + 1))
 
-        w4_raw = [None, None]
-        tab_w = [tile([P, T], I32, "tab_w%d" % a) for a in range(2)]
+        both = range(2)
+        lists = [keep.tile([P, S // 16], U16, name="list%d" % l) for l in both]
 
-        def load_w4(b, pool):
-            w4_raw[b] = pool.tile([P, 2, 2 * PASS], U8, name="w4_raw%d" % b, align_bytes=64)
-            src = w4_words.rearrange("a p n -> p a n")[:, :, 2 * PASS * b : 2 * PASS * (b + 1)]
-            nc.sync.dma_start(w4_raw[b][:].bitcast(I32), src.bitcast(I32))
+        tab_w = [tile([P, T], I32, "tab_w%d" % a) for a in both]
+        picked_s = [tile([P, 2 * S], U8, "picked_s%d" % a) for a in both]
+        picked_w = {}
+        w4_loaded = {}
+        w4_w = [tile([P, 2, 2 * PASS], U8, "w4_w%d" % b) for b in both]
+        w4_s_loaded = tile([P, 2, K], U8, "w4_s_loaded")
+        w4_s = {(a, b): tile([P, PASS], U8, "w4_s%d%d" % (a, b)) for a in both for b in both}
+        wf_loaded = {}
+        wf_bf = {(a, b): tile([P, PACK * PASS], BF16, "wf_bf%d%d" % (a, b)) for a in both for b in both}
+        wf_w = {(a, b): tile([P, PASS], U32, "wf_w%d%d" % (a, b)) for a in both for b in both}
+        wf_s = {(a, b): tile([P, PASS], U8, "wf_s%d%d" % (a, b)) for a in both for b in both}
+        h_w = {(l, b): tile([P, S], U32, "h_w%d%d" % (l, b)) for l in both for b in both}
+        h_s = {(l, b): tile([P, S], U8, "h_s%d%d" % (l, b)) for l in both for b in both}
 
-        wf_raw = [[None, None], [None, None]]
-
-        def load_tab(a):
+        def load_table_words(a):
             nc.sync.dma_start(tab_w[a][:], tab_words[a].rearrange("p t i -> p (t i)").bitcast(I32))
 
-        def load_wf(a, b, pool):
-            wf_raw[a][b] = pool.tile([P, 4, PASS], F32, name="wf_raw%d%d" % (a, b), tag="wf_raw%d%d" % (a, b), align_bytes=64)
-            src = wf[PASS * a : PASS * (a + 1), PASS * b : PASS * (b + 1)]
-            nc.sync.dma_start(wf_raw[a][b][:], src.rearrange("(p j) c -> p j c", j=4))
+        def load_w4_words(b, pool):
+            w4_loaded[b] = tile([P, 2, 2 * PASS], U8, "w4_loaded%d" % b, pool)
+            source = w4_words.rearrange("a p n -> p a n")[:, :, block(b, 2 * PASS)]
+            nc.sync.dma_start(w4_loaded[b][:].bitcast(I32), source.bitcast(I32))
 
-        w4_w = [tile([P, 2, 2 * PASS], U8, "w4_w%d" % b) for b in range(2)]
-        gs0 = tile([P, 2 * S], U8, "gs0")
-        gw = [[None, None], [None, None]]
-        gs = [gs0, gs1]
-        w4s = [[tile([P, PASS], U8, "w4s%d%d" % (a, b)) for b in range(2)] for a in range(2)]
+        def load_wf(a, b, pool):
+            wf_loaded[a, b] = tile([P, PACK, PASS], F32, "wf_loaded%d%d" % (a, b), pool)
+            source = wf[block(a, PASS), block(b, PASS)]
+            nc.sync.dma_start(wf_loaded[a, b][:], source.rearrange("(p i) c -> p i c", i=PACK))
+
+        def deal_w4_words(b):
+            nc.vector.tensor_copy(
+                w4_w[b][:].bitcast(U16).rearrange("p a (t m) -> p a t m", t=PACK),
+                w4_loaded[b][:].bitcast(U16).rearrange("p a (m t) -> p a t m", t=PACK),
+            )
 
         def deal_w4_scales(a, b):
             nc.vector.tensor_copy(
-                w4s[a][b][:].rearrange("p (t m) -> p t m", t=4),
-                w4s_raw[:, a, PASS * b : PASS * (b + 1)].rearrange("p (m t) -> p t m", t=4),
+                w4_s[a, b][:].rearrange("p (t m) -> p t m", t=PACK),
+                w4_s_loaded[:, a, block(b, PASS)].rearrange("p (m t) -> p t m", t=PACK),
             )
 
-        def deal_w4(b):
-            nc.vector.tensor_copy(
-                w4_w[b][:].bitcast(U16).rearrange("p a (t m) -> p a t m", t=4),
-                w4_raw[b][:].bitcast(U16).rearrange("p a (m t) -> p a t m", t=4),
-            )
+        def gather_words(l, a, tag=None):
+            picked_w[l, a] = tile([P, S], U32, "picked_w%d%d" % (l, a), tag=tag)
+            nc.vector.tensor_copy(picked_w[l, a][:], tab_w[a][:].bitcast(U32).indirect(lists[l][:]))
 
-        def gather_words(l, a):
-            tag = "shared" if (l, a) == (1, 0) else "gw%d%d" % (l, a)
-            gw[l][a] = keep.tile([P, S], U32, name="gw%d%d" % (l, a), tag=tag, align_bytes=64)
-            nc.vector.tensor_copy(gw[l][a][:], tab_w[a][:].bitcast(U32).indirect(lists[l][:]))
-
-        def gather_scales(l):
-            nc.vector.tensor_copy(gs0[:, S * l : S * (l + 1)], tab_s[:].indirect(lists[l][:]))
-
-        wf_il = [[keep.tile([P, 4 * PASS], BF16, name="wf_il%d%d" % (a, b), tag="wf_il%d%d" % (a, b), align_bytes=64) for b in range(2)] for a in range(2)]
-        wq_w = [[tile([P, PASS], U32, "wq_w%d%d" % (a, b)) for b in range(2)] for a in range(2)]
-        wq_s = [[tile([P, PASS], U8, "wq_s%d%d" % (a, b)) for b in range(2)] for a in range(2)]
-
-        def cast_wf(a, b, on_scalar):
-            dealt = wf_il[a][b][:].rearrange("p (t m j) -> p m j t", t=4, j=4)
-            loaded = wf_raw[a][b][:].rearrange("p j (m t) -> p m j t", t=4)
+        def shared_copy(target, source, on_scalar):
             if on_scalar > 0:
-                nc.scalar.copy(dealt[:, 0:on_scalar, :, :], loaded[:, 0:on_scalar, :, :])
+                nc.scalar.copy(target[:, 0:on_scalar, :, :], source[:, 0:on_scalar, :, :])
             if on_scalar < P:
-                nc.vector.tensor_copy(dealt[:, on_scalar:P, :, :], loaded[:, on_scalar:P, :, :])
+                nc.vector.tensor_copy(target[:, on_scalar:P, :, :], source[:, on_scalar:P, :, :])
 
-        def quantize_wf(a, b):
-            nc.vector.quantize_mx(out=wq_w[a][b][:].bitcast(FP8X4), scales=wq_s[a][b][:], in_=wf_il[a][b][:])
+        def quantize_wf(a, b, on_scalar):
+            shared_copy(
+                wf_bf[a, b][:].rearrange("p (t m i) -> p m i t", t=PACK, i=PACK),
+                wf_loaded[a, b][:].rearrange("p i (m t) -> p m i t", t=PACK),
+                on_scalar,
+            )
+            nc.vector.quantize_mx(out=wf_w[a, b][:].bitcast(FP8X4), scales=wf_s[a, b][:], in_=wf_bf[a, b][:])
 
-        def pass_w4(acc, l, a, b, t, cols, start):
+        def picked(l, a, cols):
+            return picked_w[l, a][:, cols].bitcast(FP8X4), picked_s[a][:, S * l + cols.start : S * l + cols.stop]
+
+        def mx_pass(acc, stationary, moving, start, stop):
             nc.tensor.matmul_mx(
-                out=acc,
-                lhsT=w4_w[b][:, a, 2 * P * t : 2 * P * (t + 1)].bitcast(FP4X4),
-                lhsT_scale=w4s[a][b][:, P * t : P * (t + 1)],
-                rhs=gw[l][a][:, cols].bitcast(FP8X4),
-                rhs_scale=gs[a][:, S * l + cols.start : S * l + cols.stop],
-                start=start,
-                stop=False,
+                out=acc, lhsT=stationary[0], lhsT_scale=stationary[1], rhs=moving[0], rhs_scale=moving[1], start=start, stop=stop
             )
 
-        def pass_wf(acc, l, a, b, t, cols, stop):
-            nc.tensor.matmul_mx(
-                out=acc,
-                lhsT=wq_w[a][b][:, P * t : P * (t + 1)].bitcast(FP8X4),
-                lhsT_scale=wq_s[a][b][:, P * t : P * (t + 1)],
-                rhs=gw[l][a][:, cols].bitcast(FP8X4),
-                rhs_scale=gs[a][:, S * l + cols.start : S * l + cols.stop],
-                start=False,
-                stop=stop,
-            )
+        def w4_pass(acc, l, a, b, t, cols, start):
+            weights = w4_w[b][:, a, block(t, 2 * P)].bitcast(FP4X4), w4_s[a, b][:, block(t)]
+            mx_pass(acc, weights, picked(l, a, cols), start, False)
 
-        funcs = [ACT.Abs, ACT.Relu]
-        h_il = [[None, None], [None, tile([P, 4 * S], BF16, "h_il11")]]
-        hq_w = [[tile([P, S], U32, "hq_w%d%d" % (l, b)) for b in range(2)] for l in range(2)]
-        hq_s = [[tile([P, S], U8, "hq_s%d%d" % (l, b)) for b in range(2)] for l in range(2)]
+        def wf_pass(acc, l, a, b, t, cols, stop):
+            weights = wf_w[a, b][:, block(t)].bitcast(FP8X4), wf_s[a, b][:, block(t)]
+            mx_pass(acc, weights, picked(l, a, cols), False, stop)
+
+        def quantize_traits(l, b, planes, woven, on_scalar):
+            shared_copy(
+                woven[:].rearrange("p (g i t) -> p g t i", i=PACK, t=PACK),
+                planes[:].rearrange("p t (g i) -> p g t i", i=PACK),
+                on_scalar,
+            )
+            nc.vector.quantize_mx(out=h_w[l, b][:].bitcast(FP8X4), scales=h_s[l, b][:], in_=woven[:])
+
+        trait_func = {MOVING: ACT.Abs, SEATED: ACT.Relu}
         whole = slice(0, S)
 
-        def interleave_quantize(l, b, planes, pool, tag):
-            h_il[l][b] = pool.tile([P, 4 * S], BF16, name="h_il%d%d" % (l, b), tag=tag, align_bytes=64)
-            nc.vector.tensor_copy(
-                h_il[l][b][:].rearrange("p (c i t) -> p c t i", i=4, t=4),
-                planes[:].rearrange("p t (c i) -> p c t i", i=4),
-            )
-            nc.vector.quantize_mx(out=hq_w[l][b][:].bitcast(FP8X4), scales=hq_s[l][b][:], in_=h_il[l][b][:])
-
         with tc.tile_pool(name="early", bufs=1) as early:
-            tab_s = early.tile([P, T], U8, name="tab_s", align_bytes=64)
-            nc.vector.memset(tab_s[:, 0:1536].bitcast(I32), 0)
-            nc.gpsimd.memset(tab_s[:, 1536:T].bitcast(I32), 0)
-            nc.vector.memset(w4s_raw[:].bitcast(I32), 0)
-            nc.gpsimd.memset(gs1[:].bitcast(I32), 0)
-            nc.sync.dma_start(lists[0][:], offs)
-            nc.sync.dma_start(lists[1][:], offs2)
+            tab_s = tile([P, T], U8, "tab_s", early)
+            nc.vector.memset(tab_s[:, 0:CLEAR_ON_VECTOR].bitcast(I32), 0)
+            nc.gpsimd.memset(tab_s[:, CLEAR_ON_VECTOR:T].bitcast(I32), 0)
+            nc.vector.memset(w4_s_loaded[:].bitcast(I32), 0)
+            nc.gpsimd.memset(picked_s[1][:].bitcast(I32), 0)
+            nc.sync.dma_start(lists[MOVING][:], offs)
+            nc.sync.dma_start(lists[SEATED][:], offs2)
+            load_w4_words(0, keep)
             tab_rows = tab_scales.rearrange("a (q r) t -> r q a t", r=4)
-            w4_rows = w4_scales.rearrange("a (q r) t -> r q a t", r=4)
-            warm = tile([P, 8], F32, "warm")
-            nc.vector.memset(warm[:], 0.0)
-            nc.scalar.activation(warm[:], warm[:], ACT.Sigmoid)
-
-            load_w4(0, keep)
             for r in range(4):
                 nc.sync.dma_start(tab_s[r:P:16, :].bitcast(I32), tab_rows[r].bitcast(I32))
-            load_tab(0)
+            load_table_words(0)
+            w4_rows = w4_scales.rearrange("a (q r) n -> r q a n", r=4)
             for r in range(4):
-                nc.sync.dma_start(w4s_raw[r:P:32, :, :].bitcast(I32), w4_rows[r].bitcast(I32))
+                nc.sync.dma_start(w4_s_loaded[r:P:32, :, :].bitcast(I32), w4_rows[r].bitcast(I32))
             load_wf(0, 0, keep)
-            load_tab(1)
+            load_table_words(1)
 
-            deal_w4(0)
-            gather_scales(0)
-            gather_scales(1)
+            deal_w4_words(0)
+            for l in both:
+                nc.vector.tensor_copy(picked_s[0][:, block(l, S)], tab_s[:].indirect(lists[l][:]))
+
         late = ctx.enter_context(tc.tile_pool(name="late", bufs=1))
-        nc.sync.dma_start(gs1[0 : P - 16, :].bitcast(I32), gs0[16:P, :].bitcast(I32))
+        for q in range(4):
+            nc.sync.dma_start(picked_s[1][32 * q : 32 * q + 4, :].bitcast(I32), picked_s[0][32 * q + 16 : 32 * q + 20, :].bitcast(I32))
         load_wf(1, 0, late)
-        load_w4(1, late)
+        load_w4_words(1, late)
         load_wf(0, 1, late)
         load_wf(1, 1, late)
-        gain = late.tile([P, 4], F32, name="gain")
+        gain = tile([P, 4], F32, "gain", late)
         with nc.allow_non_contiguous_dma(reason="one gain for each output row"):
             nc.sync.dma_start(gain[:], ga.rearrange("(c p) -> p c", p=P))
-        prior_sb = late.tile([P, 4, S], F32, name="prior_sb")
+        prior_sb = tile([P, 4, S], F32, "prior_sb", late)
         nc.sync.dma_start(prior_sb[:], prior.rearrange("(c p) j -> p c j", p=P))
-        gather_words(0, 0)
-        for b in range(2):
-            for a in range(2):
+
+        gather_words(MOVING, 0)
+        for b in both:
+            for a in both:
                 deal_w4_scales(a, b)
-        acc = [[bank(4 * l + t) for t in range(4)] for l in range(2)]
-        for t in range(4):
-            pass_w4(acc[0][t][:], 0, 0, 0, t, whole, True)
-        gather_words(1, 0)
-        for t in range(4):
-            pass_w4(acc[1][t][:], 1, 0, 0, t, whole, True)
-        cast_wf(0, 0, 128)
-        quantize_wf(0, 0)
-        for l in range(2):
-            for t in range(4):
-                pass_wf(acc[l][t][:], l, 0, 0, t, whole, False)
-        for l in range(2):
-            gather_words(l, 1)
-            for t in range(4):
-                pass_w4(acc[l][t][:], l, 1, 0, t, whole, False)
-        cast_wf(1, 0, 64)
-        quantize_wf(1, 0)
-        planes = [tile([P, 4, S], BF16, "planes%d" % i) for i in range(3)]
-        for l in range(2):
-            for t in range(4):
-                pass_wf(acc[l][t][:], l, 1, 0, t, whole, True)
-                nc.scalar.activation(planes[l][:, t, :], acc[l][t][:], funcs[l])
+        acc = {(l, t): bank(4 * l + t) for l in both for t in range(PACK)}
+        for t in range(PACK):
+            w4_pass(acc[MOVING, t][:], MOVING, 0, 0, t, whole, True)
+        gather_words(SEATED, 0, tag="w4_s_loaded")
+        for t in range(PACK):
+            w4_pass(acc[SEATED, t][:], SEATED, 0, 0, t, whole, True)
+        quantize_wf(0, 0, P)
+        for l in both:
+            for t in range(PACK):
+                wf_pass(acc[l, t][:], l, 0, 0, t, whole, False)
+        for l, tag in ((MOVING, "wf_loaded00"), (SEATED, "wf_bf00")):
+            gather_words(l, 1, tag)
+            for t in range(PACK):
+                w4_pass(acc[l, t][:], l, 1, 0, t, whole, False)
+        quantize_wf(1, 0, HALF)
+        planes = {l: tile([P, PACK, S], BF16, "planes%d0" % l) for l in both}
+        for l in both:
+            for t in range(PACK):
+                wf_pass(acc[l, t][:], l, 1, 0, t, whole, True)
+                nc.scalar.activation(planes[l][:, t, :], acc[l, t][:], trait_func[l])
 
-        deal_w4(1)
-        for a in range(2):
-            cast_wf(a, 1, 0)
-            quantize_wf(a, 1)
-        acc_a = [bank(t) for t in range(4)]
-        for t in range(4):
-            for a in range(2):
-                pass_w4(acc_a[t][:], 0, a, 1, t, whole, a == 0)
-        for t in range(4):
-            pass_wf(acc_a[t][:], 0, 0, 1, t, whole, False)
-        for t in range(4):
-            pass_wf(acc_a[t][:], 0, 1, 1, t, whole, True)
-            nc.scalar.activation(planes[2][:, t, :], acc_a[t][:], funcs[0])
-        interleave_quantize(1, 0, planes[1], keep, "wf_il11")
-        interleave_quantize(0, 0, planes[0], late, "wf_raw11")
+        deal_w4_words(1)
+        for a in both:
+            quantize_wf(a, 1, 0)
+        quantize_traits(SEATED, 0, planes[SEATED], tile([P, PACK * S], BF16, "woven10", keep, "wf_bf11"), 0)
+        quantize_traits(MOVING, 0, planes[MOVING], tile([P, PACK * S], BF16, "woven00", late, "wf_loaded11"), HALF)
+        acc_moving = [bank(t) for t in range(PACK)]
+        planes_moving = tile([P, PACK, S], BF16, "planes01")
+        for t in range(PACK):
+            for a in both:
+                w4_pass(acc_moving[t][:], MOVING, a, 1, t, whole, a == 0)
+        for t in range(PACK):
+            wf_pass(acc_moving[t][:], MOVING, 0, 1, t, whole, False)
+        for t in range(PACK):
+            wf_pass(acc_moving[t][:], MOVING, 1, 1, t, whole, True)
+            nc.scalar.activation(planes_moving[:, t, :], acc_moving[t][:], trait_func[MOVING])
 
-        def traits_b(c):
-            cols = slice(P * c, P * (c + 1))
-            acc_b = bank(4 + c)
-            for t in range(4):
-                part = acc_b[:, P * t : P * (t + 1)]
-                for a in range(2):
-                    pass_w4(part, 1, a, 1, t, cols, t == 0 and a == 0)
-                for a in range(2):
-                    pass_wf(part, 1, a, 1, t, cols, t == 3 and a == 1)
-            il = h_il[1][1][:, 4 * P * c : 4 * P * (c + 1)]
-            nc.scalar.activation(il.rearrange("p (n t) -> p n t", t=4), acc_b[:].rearrange("p (t n) -> p n t", t=4), funcs[1])
-            nc.vector.quantize_mx(out=hq_w[1][1][:, cols].bitcast(FP8X4), scales=hq_s[1][1][:, cols], in_=il)
-
+        woven_seated = tile([P, PACK * S], BF16, "woven11")
         second = [tile([P, S], F32, "second%d" % c) for c in range(4)]
 
+        def seated_traits(c):
+            acc_seated = bank(4 + c)
+            for t in range(PACK):
+                for a in both:
+                    w4_pass(acc_seated[:, block(t)], SEATED, a, 1, t, block(c), t == 0 and a == 0)
+                for a in both:
+                    wf_pass(acc_seated[:, block(t)], SEATED, a, 1, t, block(c), t == PACK - 1 and a == 1)
+            woven = woven_seated[:, block(c, PASS)]
+            nc.scalar.activation(
+                woven.rearrange("p (n t) -> p n t", t=PACK), acc_seated[:].rearrange("p (t n) -> p n t", t=PACK), trait_func[SEATED]
+            )
+            nc.vector.quantize_mx(out=h_w[SEATED, 1][:, block(c)].bitcast(FP8X4), scales=h_s[SEATED, 1][:, block(c)], in_=woven)
+
         def second_appeal(c):
-            cols = slice(P * c, P * (c + 1))
             e2 = bank(4 + c % 3)
-            for a in range(2):
-                nc.tensor.matmul_mx(
-                    out=e2[:],
-                    lhsT=hq_w[1][a][:, cols].bitcast(FP8X4),
-                    lhsT_scale=hq_s[1][a][:, cols],
-                    rhs=gw[0][a][:].bitcast(FP8X4),
-                    rhs_scale=gs[a][:, 0:S],
-                    start=a == 0,
-                    stop=a == 1,
-                )
+            for b in both:
+                traits = h_w[SEATED, b][:, block(c)].bitcast(FP8X4), h_s[SEATED, b][:, block(c)]
+                mx_pass(e2[:], traits, picked(MOVING, b, whole), b == 0, b == 1)
             nc.vector.tensor_tensor(second[c][:], e2[:], prior_sb[:, c, :], ALU.add)
 
-        def scores(c):
-            cols = slice(P * c, P * (c + 1))
+        def scores(c, pieces):
             e1 = bank(c)
-            for a in range(2):
-                nc.tensor.matmul_mx(
-                    out=e1[:],
-                    lhsT=gw[1][a][:, cols].bitcast(FP8X4),
-                    lhsT_scale=gs[a][:, S + P * c : S + P * (c + 1)],
-                    rhs=hq_w[0][a][:].bitcast(FP8X4),
-                    rhs_scale=hq_s[0][a][:],
-                    start=a == 0,
-                    stop=a == 1,
-                )
+            for b in both:
+                traits = h_w[MOVING, b][:].bitcast(FP8X4), h_s[MOVING, b][:]
+                mx_pass(e1[:], picked(SEATED, b, block(c)), traits, b == 0, b == 1)
             low = tile([P, S], F32, "low%d" % c)
-            res = tile([P, S], F32, "res%d" % c)
-            width = S // 2 if c == 3 else S
-            for j in range(0, S, width):
-                part = slice(j, j + width)
-                nc.vector.scalar_tensor_tensor(low[:, part], e1[:, part], gain[:, c : c + 1], second[c][:, part], ALU.mult, ALU.min)
-                nc.scalar.activation(res[:, part], low[:, part], ACT.Sigmoid)
-                nc.sync.dma_start(out[cols, part], res[:, part])
+            result = tile([P, S], F32, "result%d" % c)
+            for piece in range(pieces):
+                cols = block(piece, S // pieces)
+                nc.vector.scalar_tensor_tensor(low[:, cols], e1[:, cols], gain[:, c : c + 1], second[c][:, cols], ALU.mult, ALU.min)
+                nc.scalar.activation(result[:, cols], low[:, cols], ACT.Sigmoid)
+                nc.sync.dma_start(out[block(c), cols], result[:, cols])
 
-        traits_b(0)
-        traits_b(1)
-        interleave_quantize(0, 1, planes[2], keep, "h_il01")
-        traits_b(2)
+        seated_traits(0)
+        seated_traits(1)
+        quantize_traits(MOVING, 1, planes_moving, tile([P, PACK * S], BF16, "woven01"), 0)
+        seated_traits(2)
         second_appeal(0)
-        traits_b(3)
+        seated_traits(3)
         second_appeal(1)
-        scores(0)
+        scores(0, 1)
         second_appeal(2)
-        scores(1)
+        scores(1, 1)
         second_appeal(3)
-        scores(2)
-        scores(3)
+        scores(2, 2)
+        scores(3, 2)

from contextlib import ExitStack

import concourse.mybir as mybir

K, T, S = 1024, 2048, 512
FLOPS = 5368709120

F32 = mybir.dt.float32
BF16 = mybir.dt.bfloat16
I32 = mybir.dt.int32
U32 = mybir.dt.uint32
U16 = mybir.dt.uint16
U8 = mybir.dt.uint8
FP8X4 = mybir.dt.float8_e4m3fn_x4
FP4X4 = mybir.dt.float4_e2m1fn_x4
ACT = mybir.ActivationFunctionType
ALU = mybir.AluOpType

P = 128
PACK = 4
PASS = P * PACK
MOVING, SEATED = 0, 1
CLEAR_ON_VECTOR = 1536
HALF = P // 2


def tile_list_mutual_appeal_scores_kernel(tc, tab_words, tab_scales, offs, offs2, w4_words, w4_scales, wf, ga, prior, out):
    nc = tc.nc
    with ExitStack() as ctx:
        keep = ctx.enter_context(tc.tile_pool(name="keep", bufs=1))
        psum = ctx.enter_context(tc.psum_pool(name="psum", bufs=1))

        def tile(shape, dtype, name, pool=keep, tag=None):
            return pool.tile(shape, dtype, name=name, tag=tag or name, align_bytes=64)

        def bank(i):
            return psum.tile([P, PASS], F32, name="bank%d" % i, tag="bank%d" % i)

        def block(i, width=P):
            return slice(width * i, width * (i + 1))

        both = range(2)
        lists = [keep.tile([P, S // 16], U16, name="list%d" % l) for l in both]

        tab_w = [tile([P, T], I32, "tab_w%d" % a) for a in both]
        picked_s = [tile([P, 2 * S], U8, "picked_s%d" % a) for a in both]
        picked_w = {}
        w4_loaded = {}
        w4_w = [tile([P, 2, 2 * PASS], U8, "w4_w%d" % b) for b in both]
        w4_s_loaded = tile([P, 2, K], U8, "w4_s_loaded")
        w4_s = {(a, b): tile([P, PASS], U8, "w4_s%d%d" % (a, b)) for a in both for b in both}
        wf_loaded = {}
        wf_bf = {(a, b): tile([P, PACK * PASS], BF16, "wf_bf%d%d" % (a, b)) for a in both for b in both}
        wf_w = {(a, b): tile([P, PASS], U32, "wf_w%d%d" % (a, b)) for a in both for b in both}
        wf_s = {(a, b): tile([P, PASS], U8, "wf_s%d%d" % (a, b)) for a in both for b in both}
        h_w = {(l, b): tile([P, S], U32, "h_w%d%d" % (l, b)) for l in both for b in both}
        h_s = {(l, b): tile([P, S], U8, "h_s%d%d" % (l, b)) for l in both for b in both}

        def load_table_words(a):
            nc.sync.dma_start(tab_w[a][:], tab_words[a].rearrange("p t i -> p (t i)").bitcast(I32))

        def load_w4_words(b, pool):
            w4_loaded[b] = tile([P, 2, 2 * PASS], U8, "w4_loaded%d" % b, pool)
            source = w4_words.rearrange("a p n -> p a n")[:, :, block(b, 2 * PASS)]
            nc.sync.dma_start(w4_loaded[b][:].bitcast(I32), source.bitcast(I32))

        def load_wf(a, b, pool):
            wf_loaded[a, b] = tile([P, PACK, PASS], F32, "wf_loaded%d%d" % (a, b), pool)
            source = wf[block(a, PASS), block(b, PASS)]
            nc.sync.dma_start(wf_loaded[a, b][:], source.rearrange("(p i) c -> p i c", i=PACK))

        def deal_w4_words(b):
            nc.vector.tensor_copy(
                w4_w[b][:].bitcast(U16).rearrange("p a (t m) -> p a t m", t=PACK),
                w4_loaded[b][:].bitcast(U16).rearrange("p a (m t) -> p a t m", t=PACK),
            )

        def deal_w4_scales(a, b):
            nc.vector.tensor_copy(
                w4_s[a, b][:].rearrange("p (t m) -> p t m", t=PACK),
                w4_s_loaded[:, a, block(b, PASS)].rearrange("p (m t) -> p t m", t=PACK),
            )

        def gather_words(l, a, tag=None):
            picked_w[l, a] = tile([P, S], U32, "picked_w%d%d" % (l, a), tag=tag)
            nc.vector.tensor_copy(picked_w[l, a][:], tab_w[a][:].bitcast(U32).indirect(lists[l][:]))

        def shared_copy(target, source, on_scalar):
            if on_scalar > 0:
                nc.scalar.copy(target[:, 0:on_scalar, :, :], source[:, 0:on_scalar, :, :])
            if on_scalar < P:
                nc.vector.tensor_copy(target[:, on_scalar:P, :, :], source[:, on_scalar:P, :, :])

        def quantize_wf(a, b, on_scalar):
            shared_copy(
                wf_bf[a, b][:].rearrange("p (t m i) -> p m i t", t=PACK, i=PACK),
                wf_loaded[a, b][:].rearrange("p i (m t) -> p m i t", t=PACK),
                on_scalar,
            )
            nc.vector.quantize_mx(out=wf_w[a, b][:].bitcast(FP8X4), scales=wf_s[a, b][:], in_=wf_bf[a, b][:])

        def picked(l, a, cols):
            return picked_w[l, a][:, cols].bitcast(FP8X4), picked_s[a][:, S * l + cols.start : S * l + cols.stop]

        def mx_pass(acc, stationary, moving, start, stop):
            nc.tensor.matmul_mx(
                out=acc, lhsT=stationary[0], lhsT_scale=stationary[1], rhs=moving[0], rhs_scale=moving[1], start=start, stop=stop
            )

        def w4_pass(acc, l, a, b, t, cols, start):
            weights = w4_w[b][:, a, block(t, 2 * P)].bitcast(FP4X4), w4_s[a, b][:, block(t)]
            mx_pass(acc, weights, picked(l, a, cols), start, False)

        def wf_pass(acc, l, a, b, t, cols, stop):
            weights = wf_w[a, b][:, block(t)].bitcast(FP8X4), wf_s[a, b][:, block(t)]
            mx_pass(acc, weights, picked(l, a, cols), False, stop)

        def quantize_traits(l, b, planes, woven, on_scalar):
            shared_copy(
                woven[:].rearrange("p (g i t) -> p g t i", i=PACK, t=PACK),
                planes[:].rearrange("p t (g i) -> p g t i", i=PACK),
                on_scalar,
            )
            nc.vector.quantize_mx(out=h_w[l, b][:].bitcast(FP8X4), scales=h_s[l, b][:], in_=woven[:])

        trait_func = {MOVING: ACT.Abs, SEATED: ACT.Relu}
        whole = slice(0, S)

        with tc.tile_pool(name="early", bufs=1) as early:
            tab_s = tile([P, T], U8, "tab_s", early)
            nc.vector.memset(tab_s[:, 0:CLEAR_ON_VECTOR].bitcast(I32), 0)
            nc.gpsimd.memset(tab_s[:, CLEAR_ON_VECTOR:T].bitcast(I32), 0)
            nc.vector.memset(w4_s_loaded[:].bitcast(I32), 0)
            nc.gpsimd.memset(picked_s[1][:].bitcast(I32), 0)
            nc.sync.dma_start(lists[MOVING][:], offs)
            nc.sync.dma_start(lists[SEATED][:], offs2)
            load_w4_words(0, keep)
            tab_rows = tab_scales.rearrange("a (q r) t -> r q a t", r=4)
            for r in range(4):
                nc.sync.dma_start(tab_s[r:P:16, :].bitcast(I32), tab_rows[r].bitcast(I32))
            load_table_words(0)
            w4_rows = w4_scales.rearrange("a (q r) n -> r q a n", r=4)
            for r in range(4):
                nc.sync.dma_start(w4_s_loaded[r:P:32, :, :].bitcast(I32), w4_rows[r].bitcast(I32))
            load_wf(0, 0, keep)
            load_table_words(1)

            deal_w4_words(0)
            for l in both:
                nc.vector.tensor_copy(picked_s[0][:, block(l, S)], tab_s[:].indirect(lists[l][:]))

        late = ctx.enter_context(tc.tile_pool(name="late", bufs=1))
        for q in range(4):
            nc.sync.dma_start(picked_s[1][32 * q : 32 * q + 4, :].bitcast(I32), picked_s[0][32 * q + 16 : 32 * q + 20, :].bitcast(I32))
        load_wf(1, 0, late)
        load_w4_words(1, late)
        load_wf(0, 1, late)
        load_wf(1, 1, late)
        gain = tile([P, 4], F32, "gain", late)
        with nc.allow_non_contiguous_dma(reason="one gain for each output row"):
            nc.sync.dma_start(gain[:], ga.rearrange("(c p) -> p c", p=P))
        prior_sb = tile([P, 4, S], F32, "prior_sb", late)
        nc.sync.dma_start(prior_sb[:], prior.rearrange("(c p) j -> p c j", p=P))

        gather_words(MOVING, 0)
        for b in both:
            for a in both:
                deal_w4_scales(a, b)
        acc = {(l, t): bank(4 * l + t) for l in both for t in range(PACK)}
        for t in range(PACK):
            w4_pass(acc[MOVING, t][:], MOVING, 0, 0, t, whole, True)
        gather_words(SEATED, 0, tag="w4_s_loaded")
        for t in range(PACK):
            w4_pass(acc[SEATED, t][:], SEATED, 0, 0, t, whole, True)
        quantize_wf(0, 0, P)
        for l in both:
            for t in range(PACK):
                wf_pass(acc[l, t][:], l, 0, 0, t, whole, False)
        for l, tag in ((MOVING, "wf_loaded00"), (SEATED, "wf_bf00")):
            gather_words(l, 1, tag)
            for t in range(PACK):
                w4_pass(acc[l, t][:], l, 1, 0, t, whole, False)
        quantize_wf(1, 0, HALF)
        planes = {l: tile([P, PACK, S], BF16, "planes%d0" % l) for l in both}
        for l in both:
            for t in range(PACK):
                wf_pass(acc[l, t][:], l, 1, 0, t, whole, True)
                nc.scalar.activation(planes[l][:, t, :], acc[l, t][:], trait_func[l])

        deal_w4_words(1)
        for a in both:
            quantize_wf(a, 1, 0)
        quantize_traits(SEATED, 0, planes[SEATED], tile([P, PACK * S], BF16, "woven10", keep, "wf_bf11"), 0)
        quantize_traits(MOVING, 0, planes[MOVING], tile([P, PACK * S], BF16, "woven00", late, "wf_loaded11"), HALF)
        acc_moving = [bank(t) for t in range(PACK)]
        planes_moving = tile([P, PACK, S], BF16, "planes01")
        for t in range(PACK):
            for a in both:
                w4_pass(acc_moving[t][:], MOVING, a, 1, t, whole, a == 0)
        for t in range(PACK):
            wf_pass(acc_moving[t][:], MOVING, 0, 1, t, whole, False)
        for t in range(PACK):
            wf_pass(acc_moving[t][:], MOVING, 1, 1, t, whole, True)
            nc.scalar.activation(planes_moving[:, t, :], acc_moving[t][:], trait_func[MOVING])

        woven_seated = tile([P, PACK * S], BF16, "woven11")
        second = [tile([P, S], F32, "second%d" % c) for c in range(4)]

        def seated_traits(c):
            acc_seated = bank(4 + c)
            for t in range(PACK):
                for a in both:
                    w4_pass(acc_seated[:, block(t)], SEATED, a, 1, t, block(c), t == 0 and a == 0)
                for a in both:
                    wf_pass(acc_seated[:, block(t)], SEATED, a, 1, t, block(c), t == PACK - 1 and a == 1)
            woven = woven_seated[:, block(c, PASS)]
            nc.scalar.activation(
                woven.rearrange("p (n t) -> p n t", t=PACK), acc_seated[:].rearrange("p (t n) -> p n t", t=PACK), trait_func[SEATED]
            )
            nc.vector.quantize_mx(out=h_w[SEATED, 1][:, block(c)].bitcast(FP8X4), scales=h_s[SEATED, 1][:, block(c)], in_=woven)

        def second_appeal(c):
            e2 = bank(4 + c % 3)
            for b in both:
                traits = h_w[SEATED, b][:, block(c)].bitcast(FP8X4), h_s[SEATED, b][:, block(c)]
                mx_pass(e2[:], traits, picked(MOVING, b, whole), b == 0, b == 1)
            nc.vector.tensor_tensor(second[c][:], e2[:], prior_sb[:, c, :], ALU.add)

        def scores(c, pieces):
            e1 = bank(c)
            for b in both:
                traits = h_w[MOVING, b][:].bitcast(FP8X4), h_s[MOVING, b][:]
                mx_pass(e1[:], picked(SEATED, b, block(c)), traits, b == 0, b == 1)
            low = tile([P, S], F32, "low%d" % c)
            result = tile([P, S], F32, "result%d" % c)
            for piece in range(pieces):
                cols = block(piece, S // pieces)
                nc.vector.scalar_tensor_tensor(low[:, cols], e1[:, cols], gain[:, c : c + 1], second[c][:, cols], ALU.mult, ALU.min)
                nc.scalar.activation(result[:, cols], low[:, cols], ACT.Sigmoid)
                nc.sync.dma_start(out[block(c), cols], result[:, cols])

        seated_traits(0)
        seated_traits(1)
        quantize_traits(MOVING, 1, planes_moving, tile([P, PACK * S], BF16, "woven01"), 0)
        seated_traits(2)
        second_appeal(0)
        seated_traits(3)
        second_appeal(1)
        scores(0, 1)
        second_appeal(2)
        scores(1, 1)
        second_appeal(3)
        scores(2, 2)
        scores(3, 2)
